import numpy as np
import ml_dtypes


def mxq(x, axis, fmt="e4m3"):
    dtype, down = {"e4m3": (ml_dtypes.float8_e4m3fn, 7), "e5m2": (ml_dtypes.float8_e5m2, 14)}[fmt]
    v = np.moveaxis(np.asarray(x, np.float32).astype(ml_dtypes.bfloat16).astype(np.float64), axis, -1)
    blocks = v.reshape(v.shape[:-1] + (-1, 32))
    amax = np.abs(blocks).max(-1, keepdims=True)
    byte = np.maximum(np.where(amax > 0, np.frexp(amax)[1] - 1 + 127, 0) - down, 1)
    scale = np.exp2(byte - 127.0)
    codes = (blocks / scale).astype(np.float32).astype(dtype).astype(np.float64)
    return np.moveaxis((codes * scale).reshape(v.shape), -1, axis)


WIDE = False


def mx_kscale(k):
    if not WIDE:
        return np.ones(k)
    levels = np.array([10, -10, 5, -5, 0])
    if k % 512:
        return np.exp2(np.random.permutation(np.resize(levels, k // 32))).repeat(32)
    a = np.empty((k // 512, 16))
    for p in range(k // 512):
        a[p, :8] = np.random.permutation(np.resize(levels, 8))
        for g in range(8):
            far = levels[np.abs(levels - a[p, g]) >= 10]
            a[p, g + 8] = far[np.random.randint(len(far))]
    return np.exp2(a.ravel()).repeat(32)


def f64(x):
    return np.asarray(x).astype(np.float64)


def striped(idx):
    return np.tile(idx.reshape(-1, 16).T, (8, 1)).astype(np.uint16)


def unstriped(offs):
    return offs[:16].T.reshape(-1).astype(np.int64)


def striped8(idx):
    return np.concatenate([x.reshape(-1, 16).T for x in idx]).astype(np.uint16)


def runs(offs, k):
    lists = np.stack([offs[16 * r : 16 * r + 16].T.reshape(-1) for r in range(8)]).astype(np.int64)
    return lists[np.arange(k) % 512 // 64]


def pack_weight(w):
    k, n = w.shape
    w = f64(np.asarray(w, np.float32).astype(ml_dtypes.bfloat16)).reshape(k // 32, 32, n)
    amax = np.abs(w).max(1)
    byte = np.clip(np.where(amax > 0, np.frexp(amax)[1] - 1 + 127 - 7, 1), 1, 254)
    scaled = (w * np.exp2(127.0 - byte)[:, None, :]).reshape(k, n).astype(np.float32)
    words = np.ascontiguousarray(scaled.reshape(k // 512, 128, 4, n).transpose(0, 1, 3, 2)).astype(ml_dtypes.float8_e4m3fn).view(np.uint8)
    return words, np.ascontiguousarray(byte.astype(np.uint8).reshape(k // 512, 16, n))


def unpack_weight(words, scales):
    g, p, n, _ = words.shape
    vals = np.ascontiguousarray(words).view(ml_dtypes.float8_e4m3fn).astype(np.float64) * np.repeat(np.exp2(scales.astype(np.float64) - 127.0), 8, axis=1)[..., None]
    return vals.transpose(0, 1, 3, 2).reshape(g * 512, n)


E2M1 = np.array([0.0, 0.5, 1.0, 1.5, 2.0, 3.0, 4.0, 6.0, -0.0, -0.5, -1.0, -1.5, -2.0, -3.0, -4.0, -6.0])


def pack_fp4(w):
    k, n = w.shape
    w = f64(np.asarray(w, np.float32).astype(ml_dtypes.bfloat16)).reshape(k // 32, 32, n)
    amax = np.abs(w).max(1)
    mant, ex = np.frexp(amax / 6.0)
    byte = np.clip(np.where(amax > 0, np.where(mant > 0.5, ex, ex - 1) + 127, 1), 1, 254)
    scaled = (w * np.exp2(127.0 - byte)[:, None, :]).reshape(k, n).astype(np.float32)
    c = np.ascontiguousarray(scaled.reshape(k // 512, 128, 4, n).transpose(0, 1, 3, 2)).astype(ml_dtypes.float4_e2m1fn).view(np.uint8) & 0xF
    words = (c[..., 0::2] | (c[..., 1::2] << 4)).reshape(k // 512, 128, 2 * n)
    return np.ascontiguousarray(words), np.ascontiguousarray(byte.astype(np.uint8).reshape(k // 512, 16, n))


def unpack_fp4(words, scales):
    g, _, n = scales.shape
    words = np.ascontiguousarray(words).reshape(g, 128, n, 2)
    nib = np.empty((g, 128, n, 4), np.uint8)
    nib[..., 0::2] = words & 0xF
    nib[..., 1::2] = words >> 4
    vals = E2M1[nib] * np.repeat(np.exp2(scales.astype(np.float64) - 127.0), 8, axis=1)[..., None]
    return vals.transpose(0, 1, 3, 2).reshape(g * 512, n)


def planes(y):
    n, m = y.shape
    v = y.astype(np.float32).astype(ml_dtypes.bfloat16).astype(np.float64).reshape(n // 32, 32, m)
    top = np.abs(v).max(1)
    byte = np.clip(np.where(top > 0, np.frexp(top)[1] - 1 + 127 - 7, 1), 1, 254)
    codes = (v * np.exp2(127.0 - byte)[:, None, :]).reshape(n, m).astype(np.float32).astype(ml_dtypes.float8_e4m3fn).view(np.uint8)
    words = codes.reshape(n // 512, 128, 4, m).transpose(0, 1, 3, 2)
    return np.ascontiguousarray(words), np.ascontiguousarray(byte.astype(np.uint8).reshape(n // 512, 16, m))


K, T, S, H, C = 512, 2048, 512, 512, 512


def setup_inputs():
    n = np.random.standard_normal
    s = mx_kscale(K)[:, None]
    packed_xT = pack_weight(n((K, T)) * s)
    packed_w1 = pack_fp4(n((K, H)) / np.sqrt(K) / s)
    packed_w2 = pack_fp4(n((K, H)) / np.sqrt(K) / s)
    return {
        "x_words": packed_xT[0],
        "x_scales": packed_xT[1],
        "w1_words": packed_w1[0],
        "w1_scales": packed_w1[1],
        "w2_words": packed_w2[0],
        "w2_scales": packed_w2[1],
        "gs": (np.random.uniform(0.5, 1.5, (K, 1)) / s).astype(np.float32),
        "offs": striped(np.random.permutation(T)[:S]),
        "two": striped(np.random.permutation(T)[:S]),
        "lf": striped8(np.stack([np.random.permutation(S) for _ in range(8)])),
        "rt": striped8(np.stack([np.random.permutation(S) for _ in range(8)])),
        "cand": striped(np.random.permutation(T)[:C]),
    }


def reference(x_words, x_scales, w1_words, w1_scales, w2_words, w2_scales, gs, offs, two, lf, rt, cand):
    x_cand = unpack_weight(x_words, x_scales)[:, unstriped(cand)]
    x_two = unpack_weight(x_words, x_scales)[:, unstriped(two)]
    c = unpack_fp4(w2_words, w2_scales).T @ x_two
    xq = unpack_weight(x_words, x_scales)[:, unstriped(offs)]
    y = unpack_fp4(w1_words, w1_scales).T @ xq
    e2 = y + 0.5 * (c - (c[np.arange(H)[:, None], runs(lf, H)]))
    z = f64(gs) * (c + 0.5 * (e2[np.arange(H)[:, None], runs(rt, H)] - e2))
    out_0 = 0.0625 * ((x_cand.T @ mxq(z, 0, "e4m3")))
    return (out_0,) + planes(out_0)

@@ -1,0 +1,221 @@
+from contextlib import ExitStack
+
+import concourse.mybir as mybir
+
+K, T, S, H, C = 512, 2048, 512, 512, 512
+FLOPS = 2 * K * H * S * 2 + 2 * K * C * S
+
+F32 = mybir.dt.float32
+BF16 = mybir.dt.bfloat16
+I32 = mybir.dt.int32
+U32 = mybir.dt.uint32
+U16 = mybir.dt.uint16
+U8 = mybir.dt.uint8
+FP8X4 = mybir.dt.float8_e4m3fn_x4
+FP4X4 = mybir.dt.float4_e2m1fn_x4
+MULT = mybir.AluOpType.mult
+ADD = mybir.AluOpType.add
+SUB = mybir.AluOpType.subtract
+COPY = mybir.ActivationFunctionType.Copy
+
+P = 128
+PACK = 4
+QUADS = 4
+LIST_ROWS = 16
+HALF = 256
+CHUNK = 128
+
+
+def tile_picked_fdtd8_none_po_kernel(
+    tc, x_words, x_scales, w1_words, w1_scales, w2_words, w2_scales, gs, offs, two, lf, rt, cand, out_0, out_1, out_2
+):
+    nc = tc.nc
+    with ExitStack() as ctx:
+        keep = ctx.enter_context(tc.tile_pool(name="keep", bufs=1))
+        psum = ctx.enter_context(tc.psum_pool(name="psum", bufs=1))
+
+        def sb(name, shape, dtype):
+            return keep.tile(shape, dtype, name=name, align_bytes=64)
+
+        def load_list(name, src):
+            t = keep.tile([P, S // LIST_ROWS], U16, name=name)
+            nc.sync.dma_start(t[:], src)
+            return t
+
+        def load_scales(name, src, width, zero_engine, queue):
+            t = sb(name, [P, width], U8)
+            zero_engine.memset(t[:].bitcast(I32), 0)
+            for q in range(QUADS):
+                queue.dma_start(t[32 * q : 32 * q + 4, :].bitcast(I32), src[0, 4 * q : 4 * q + 4, :].bitcast(I32))
+            return t
+
+        def load_w_words(name, src):
+            t = sb(name, [P, 2 * H], U8)
+            nc.sync.dma_start(t[:].bitcast(I32), src[0].bitcast(I32))
+            return t
+
+        xs = load_scales("xs", x_scales, T, nc.vector, nc.scalar)
+        two_l = load_list("two_l", two)
+        offs_l = load_list("offs_l", offs)
+        w2w = load_w_words("w2w", w2_words)
+        xw = sb("xw", [P, T], U32)
+        nc.sync.dma_start(xw[:].bitcast(I32), x_words[0].rearrange("p n t -> p (n t)").bitcast(I32))
+        w2s = load_scales("w2s", w2_scales, H, nc.gpsimd, nc.sync)
+        gs_t = sb("gs_t", [P, PACK], F32)
+        nc.sync.dma_start(gs_t[:], gs.rearrange("(p t) o -> p (t o)", t=PACK))
+        w1w = load_w_words("w1w", w1_words)
+        w1s = load_scales("w1s", w1_scales, H, nc.gpsimd, nc.sync)
+        cand_l = load_list("cand_l", cand)
+        lf_l = load_list("lf_l", lf)
+        rt_l = load_list("rt_l", rt)
+
+        gs_c = sb("gs_c", [P, PACK], F32)
+        gs_y = sb("gs_y", [P, PACK], F32)
+        nc.scalar.mul(gs_c[:], gs_t[:], -0.25)
+        nc.scalar.mul(gs_y[:], gs_t[:], 0.5)
+
+        def gather_bytes(name, lst):
+            t = sb(name, [P, S], U8)
+            nc.vector.tensor_copy(t[:], xs[:].indirect(lst[:]))
+            return t
+
+        def gather_words(name, lst):
+            t = sb(name, [P, S], U32)
+            nc.vector.tensor_copy(t[:], xw[:].indirect(lst[:]))
+            return t
+
+        def deal_bytes(name, src):
+            t = sb(name, [P, H], U8)
+            nc.vector.tensor_copy(
+                t[:].rearrange("p (t m) -> p t m", t=PACK), src[:].rearrange("p (m t) -> p t m", t=PACK)
+            )
+            return t
+
+        def deal_fp4(name, src):
+            t = sb(name, [P, 2 * H], U8)
+            nc.vector.tensor_copy(
+                t[:].rearrange("p (t m b) -> p t m b", t=PACK, b=2),
+                src[:].rearrange("p (m t b) -> p t m b", t=PACK, b=2),
+            )
+            return t
+
+        def project(tag0, w_words, w_scales, xg_words, xg_scales):
+            banks = []
+            for t in range(PACK):
+                bank = psum.tile([P, S], F32, name="bank%d" % (tag0 + t), tag="bank%d" % (tag0 + t))
+                nc.tensor.matmul_mx(
+                    out=bank[:],
+                    lhsT=w_words[:, 2 * P * t : 2 * P * (t + 1)].bitcast(FP4X4),
+                    lhsT_scale=w_scales[:, P * t : P * (t + 1)],
+                    rhs=xg_words[:].bitcast(FP8X4),
+                    rhs_scale=xg_scales[:],
+                    start=True,
+                    stop=True,
+                )
+                banks.append(bank)
+            return banks
+
+        two_s = gather_bytes("two_s", two_l)
+        offs_s = gather_bytes("offs_s", offs_l)
+        w2w_d = deal_fp4("w2w_d", w2w)
+        w2s_d = deal_bytes("w2s_d", w2s)
+        two_w = gather_words("two_w", two_l)
+        c_ps = project(0, w2w_d, w2s_d, two_w, two_s)
+        cq = []
+        for t in range(PACK):
+            w = sb("cq%d" % t, [P, S], F32)
+            nc.scalar.activation(w[:], c_ps[t][:], COPY, scale=gs_c[:, t : t + 1])
+            cq.append(w)
+        w1w_d = deal_fp4("w1w_d", w1w)
+        w1s_d = deal_bytes("w1s_d", w1s)
+        offs_w = gather_words("offs_w", offs_l)
+        y_ps = project(PACK, w1w_d, w1s_d, offs_w, offs_s)
+        cand_s = gather_bytes("cand_s", cand_l)
+        cand_w_d = sb("cand_w_d", [P, C], U32)
+        nc.vector.tensor_copy(cand_w_d[:].rearrange("p (t m) -> p m t", t=PACK), xw[:].indirect(cand_l[:]))
+        cand_s_d = deal_bytes("cand_s_d", cand_s)
+
+        own = [sb("own%d" % t, [P, S], F32) for t in range(PACK)]
+        eh = [sb("eh%d" % t, [P, S], F32) for t in range(PACK)]
+        rest = [sb("rest%d" % t, [P, S], F32) for t in range(PACK)]
+
+        def make_own(t):
+            nc.vector.scalar_tensor_tensor(own[t][:], y_ps[t][:], gs_y[:, t : t + 1], cq[t][:], MULT, SUB)
+
+        def make_e(t):
+            for h in range(S // HALF):
+                cols = slice(h * HALF, (h + 1) * HALF)
+                lcols = slice(h * HALF // LIST_ROWS, (h + 1) * HALF // LIST_ROWS)
+                nc.vector.tensor_tensor(eh[t][:, cols], cq[t][:].indirect(lf_l[:, lcols]), own[t][:, cols], ADD)
+
+        def make_rest(t):
+            nc.vector.scalar_tensor_tensor(rest[t][:], cq[t][:], -4.0, eh[t][:], MULT, SUB)
+
+        make_own(0)
+        for t in range(PACK):
+            if t + 1 < PACK:
+                make_own(t + 1)
+            make_e(t)
+            if t > 0:
+                make_rest(t - 1)
+        make_rest(PACK - 1)
+
+        n_chunks = S // CHUNK
+        out_rows = out_0.rearrange("(p t) j -> p t j", t=PACK)
+        out_words = out_1[0].rearrange("p n t -> p (n t)").bitcast(I32)
+        ow = sb("ow", [P, S], U32)
+        osc = sb("osc", [P, S], U8)
+        zf = [sb("zf%d" % q, [P, PACK, CHUNK], F32) for q in range(n_chunks)]
+        zb = [sb("zb%d" % q, [P, CHUNK, PACK], BF16) for q in range(n_chunks)]
+        zw = [sb("zw%d" % q, [P, CHUNK], U32) for q in range(n_chunks)]
+        zs = [sb("zs%d" % q, [P, CHUNK], U8) for q in range(n_chunks)]
+        of = [sb("of%d" % q, [P, PACK, CHUNK], F32) for q in range(n_chunks)]
+        ob = [sb("ob%d" % q, [P, CHUNK, PACK], BF16) for q in range(n_chunks)]
+
+        def weave(engine_copy, dst, src):
+            engine_copy(dst[:].rearrange("p (c i) t -> p c t i", i=4), src[:].rearrange("p t (c i) -> p c t i", i=4))
+
+        def z_gather(q):
+            cols = slice(q * CHUNK, (q + 1) * CHUNK)
+            lcols = slice(q * CHUNK // LIST_ROWS, (q + 1) * CHUNK // LIST_ROWS)
+            for t in range(PACK):
+                nc.vector.tensor_tensor(zf[q][:, t, :], eh[t][:].indirect(rt_l[:, lcols]), rest[t][:, cols], ADD)
+            weave(nc.scalar.copy if q < n_chunks - 1 else nc.vector.tensor_copy, zb[q], zf[q])
+
+        def score(q):
+            cols = slice(q * CHUNK, (q + 1) * CHUNK)
+            nc.vector.quantize_mx(
+                out=zw[q][:].bitcast(FP8X4), scales=zs[q][:], in_=zb[q][:].rearrange("p j t -> p (j t)")
+            )
+            bank = psum.tile([P, PACK, CHUNK], F32, name="obank%d" % q, tag="bank%d" % q)
+            for t in range(PACK):
+                nc.tensor.matmul_mx(
+                    out=bank[:, t, :],
+                    lhsT=cand_w_d[:, P * t : P * (t + 1)].bitcast(FP8X4),
+                    lhsT_scale=cand_s_d[:, P * t : P * (t + 1)],
+                    rhs=zw[q][:].bitcast(FP8X4),
+                    rhs_scale=zs[q][:],
+                    start=True,
+                    stop=True,
+                )
+            nc.scalar.activation(of[q][:], bank[:], COPY, scale=0.0625)
+            nc.sync.dma_start(out_rows[:, :, cols], of[q][:])
+            weave(nc.scalar.copy if q < 1 else nc.vector.tensor_copy, ob[q], of[q])
+
+        def hand_on(q):
+            cols = slice(q * CHUNK, (q + 1) * CHUNK)
+            nc.vector.quantize_mx(
+                out=ow[:, cols].bitcast(FP8X4), scales=osc[:, cols], in_=ob[q][:].rearrange("p j t -> p (j t)")
+            )
+            nc.sync.dma_start(out_words[:, cols], ow[:, cols].bitcast(I32))
+
+        for step in range(n_chunks + 2):
+            if step < n_chunks:
+                z_gather(step)
+            if 0 <= step - 1 < n_chunks:
+                score(step - 1)
+            if 0 <= step - 2 < n_chunks:
+                hand_on(step - 2)
+        for q in range(QUADS):
+            queue = nc.sync if q % 2 == 0 else nc.scalar
+            queue.dma_start(out_2[0, 4 * q : 4 * q + 4, :].bitcast(I32), osc[32 * q : 32 * q + 4, :].bitcast(I32))

@@ -1,6 +1,7 @@
 from contextlib import ExitStack
 
 import concourse.mybir as mybir
+from concourse.masks import make_identity
 
 K, T, S, H, C = 512, 2048, 512, 512, 512
 FLOPS = 2 * K * H * S * 2 + 2 * K * C * S
@@ -24,6 +25,7 @@ QUADS = 4
 LIST_ROWS = 16
 HALF = 256
 CHUNK = 128
+PE_TILES = 3
 
 
 def tile_picked_fdtd8_none_po_kernel(
@@ -34,8 +36,8 @@ def tile_picked_fdtd8_none_po_kernel(
         keep = ctx.enter_context(tc.tile_pool(name="keep", bufs=1))
         psum = ctx.enter_context(tc.psum_pool(name="psum", bufs=1))
 
-        def sb(name, shape, dtype):
-            return keep.tile(shape, dtype, name=name, align_bytes=64)
+        def sb(name, shape, dtype, tag=None):
+            return keep.tile(shape, dtype, name=name, tag=tag or name, align_bytes=64)
 
         def load_list(name, src):
             t = keep.tile([P, S // LIST_ROWS], U16, name=name)
@@ -44,27 +46,29 @@ def tile_picked_fdtd8_none_po_kernel(
 
         def load_scales(name, src, width, zero_engine, queue):
             t = sb(name, [P, width], U8)
-            zero_engine.memset(t[:].bitcast(I32), 0)
+            share = width // len(zero_engine)
+            for i, engine in enumerate(zero_engine):
+                engine.memset(t[:, i * share : (i + 1) * share].bitcast(I32), 0)
             for q in range(QUADS):
-                queue.dma_start(t[32 * q : 32 * q + 4, :].bitcast(I32), src[0, 4 * q : 4 * q + 4, :].bitcast(I32))
+                queue[q % len(queue)].dma_start(t[32 * q : 32 * q + 4, :].bitcast(I32), src[0, 4 * q : 4 * q + 4, :].bitcast(I32))
             return t
 
-        def load_w_words(name, src):
+        def load_w_words(name, src, queue):
             t = sb(name, [P, 2 * H], U8)
-            nc.sync.dma_start(t[:].bitcast(I32), src[0].bitcast(I32))
+            queue.dma_start(t[:].bitcast(I32), src[0].bitcast(I32))
             return t
 
-        xs = load_scales("xs", x_scales, T, nc.vector, nc.scalar)
+        xs = load_scales("xs", x_scales, T, [nc.vector, nc.gpsimd], [nc.scalar, nc.sync])
         two_l = load_list("two_l", two)
         offs_l = load_list("offs_l", offs)
-        w2w = load_w_words("w2w", w2_words)
+        w2w = load_w_words("w2w", w2_words, nc.scalar)
         xw = sb("xw", [P, T], U32)
         nc.sync.dma_start(xw[:].bitcast(I32), x_words[0].rearrange("p n t -> p (n t)").bitcast(I32))
-        w2s = load_scales("w2s", w2_scales, H, nc.gpsimd, nc.sync)
+        w2s = load_scales("w2s", w2_scales, H, [nc.vector], [nc.sync])
+        w1w = load_w_words("w1w", w1_words, nc.sync)
         gs_t = sb("gs_t", [P, PACK], F32)
         nc.sync.dma_start(gs_t[:], gs.rearrange("(p t) o -> p (t o)", t=PACK))
-        w1w = load_w_words("w1w", w1_words)
-        w1s = load_scales("w1s", w1_scales, H, nc.gpsimd, nc.sync)
+        w1s = load_scales("w1s", w1_scales, H, [nc.vector], [nc.sync])
         cand_l = load_list("cand_l", cand)
         lf_l = load_list("lf_l", lf)
         rt_l = load_list("rt_l", rt)
@@ -72,15 +76,19 @@ def tile_picked_fdtd8_none_po_kernel(
         gs_c = sb("gs_c", [P, PACK], F32)
         gs_y = sb("gs_y", [P, PACK], F32)
         nc.scalar.mul(gs_c[:], gs_t[:], -0.25)
-        nc.scalar.mul(gs_y[:], gs_t[:], 0.5)
+        gs_n = sb("gs_n", [P, PACK], F32)
+        nc.scalar.mul(gs_y[:], gs_t[:], -0.5)
+        nc.scalar.mul(gs_n[:], gs_t[:], -1.0)
+        ident = sb("ident", [P, P], F32)
+        make_identity(nc, ident[:])
 
-        def gather_bytes(name, lst):
-            t = sb(name, [P, S], U8)
+        def gather_bytes(name, lst, tag=None):
+            t = sb(name, [P, S], U8, tag)
             nc.vector.tensor_copy(t[:], xs[:].indirect(lst[:]))
             return t
 
-        def gather_words(name, lst):
-            t = sb(name, [P, S], U32)
+        def gather_words(name, lst, tag=None):
+            t = sb(name, [P, S], U32, tag)
             nc.vector.tensor_copy(t[:], xw[:].indirect(lst[:]))
             return t
 
@@ -94,8 +102,8 @@ def tile_picked_fdtd8_none_po_kernel(
         def deal_fp4(name, src):
             t = sb(name, [P, 2 * H], U8)
             nc.vector.tensor_copy(
-                t[:].rearrange("p (t m b) -> p t m b", t=PACK, b=2),
-                src[:].rearrange("p (m t b) -> p t m b", t=PACK, b=2),
+                t[:].bitcast(U16).rearrange("p (t m) -> p t m", t=PACK),
+                src[:].bitcast(U16).rearrange("p (m t) -> p t m", t=PACK),
             )
             return t
 
@@ -115,20 +123,25 @@ def tile_picked_fdtd8_none_po_kernel(
                 banks.append(bank)
             return banks
 
+        w2w_d = deal_fp4("w2w_d", w2w)
         two_s = gather_bytes("two_s", two_l)
         offs_s = gather_bytes("offs_s", offs_l)
-        w2w_d = deal_fp4("w2w_d", w2w)
-        w2s_d = deal_bytes("w2s_d", w2s)
         two_w = gather_words("two_w", two_l)
+        w2s_d = deal_bytes("w2s_d", w2s)
         c_ps = project(0, w2w_d, w2s_d, two_w, two_s)
         cq = []
         for t in range(PACK):
             w = sb("cq%d" % t, [P, S], F32)
             nc.scalar.activation(w[:], c_ps[t][:], COPY, scale=gs_c[:, t : t + 1])
             cq.append(w)
+        cn = []
+        for t in range(PE_TILES):
+            w = sb("cn%d" % t, [P, S], F32)
+            nc.scalar.activation(w[:], c_ps[t][:], COPY, scale=gs_n[:, t : t + 1])
+            cn.append(w)
         w1w_d = deal_fp4("w1w_d", w1w)
+        offs_w = gather_words("offs_w", offs_l, "w2s")
         w1s_d = deal_bytes("w1s_d", w1s)
-        offs_w = gather_words("offs_w", offs_l)
         y_ps = project(PACK, w1w_d, w1s_d, offs_w, offs_s)
         cand_s = gather_bytes("cand_s", cand_l)
         cand_w_d = sb("cand_w_d", [P, C], U32)
@@ -140,54 +153,88 @@ def tile_picked_fdtd8_none_po_kernel(
         rest = [sb("rest%d" % t, [P, S], F32) for t in range(PACK)]
 
         def make_own(t):
-            nc.vector.scalar_tensor_tensor(own[t][:], y_ps[t][:], gs_y[:, t : t + 1], cq[t][:], MULT, SUB)
+            nc.vector.scalar_tensor_tensor(own[t][:], y_ps[t][:], gs_y[:, t : t + 1], cq[t][:], MULT, ADD)
+
+        def rest_by_transposes(t, h):
+            blocks = HALF // P
+            turned_ps = psum.tile([P, blocks, P], F32, name="turn%d_%d" % (t, h), tag="bank%d" % h)
+            for b in range(blocks):
+                cols = slice(h * HALF + b * P, h * HALF + (b + 1) * P)
+                nc.tensor.matmul(turned_ps[:, b, :], cn[t][:, cols], ident[:], is_transpose=True, start=True, stop=False)
+                nc.tensor.matmul(turned_ps[:, b, :], eh[t][:, cols], ident[:], is_transpose=True, start=False, stop=True)
+            turned = sb("turned%d_%d" % (t, h), [P, blocks, P], F32)
+            nc.scalar.copy(turned[:], turned_ps[:])
+            back_ps = psum.tile([P, blocks, P], F32, name="back%d_%d" % (t, h), tag="bank%d" % (2 + h))
+            for b in range(blocks):
+                nc.tensor.transpose(back_ps[:, b, :], turned[:, b, :], ident[:])
+            nc.scalar.copy(rest[t][:, h * HALF : (h + 1) * HALF], back_ps[:].rearrange("p b j -> p (b j)"))
 
         def make_e(t):
             for h in range(S // HALF):
                 cols = slice(h * HALF, (h + 1) * HALF)
                 lcols = slice(h * HALF // LIST_ROWS, (h + 1) * HALF // LIST_ROWS)
-                nc.vector.tensor_tensor(eh[t][:, cols], cq[t][:].indirect(lf_l[:, lcols]), own[t][:, cols], ADD)
+                nc.vector.tensor_tensor(eh[t][:, cols], cq[t][:].indirect(lf_l[:, lcols]), own[t][:, cols], SUB)
+                if t < PE_TILES:
+                    rest_by_transposes(t, h)
 
         def make_rest(t):
-            nc.vector.scalar_tensor_tensor(rest[t][:], cq[t][:], -4.0, eh[t][:], MULT, SUB)
+            for h in range(S // HALF):
+                cols = slice(h * HALF, (h + 1) * HALF)
+                nc.vector.scalar_tensor_tensor(rest[t][:, cols], cq[t][:, cols], 4.0, eh[t][:, cols], MULT, ADD)
 
         make_own(0)
         for t in range(PACK):
             if t + 1 < PACK:
                 make_own(t + 1)
             make_e(t)
-            if t > 0:
-                make_rest(t - 1)
-        make_rest(PACK - 1)
+        for t in range(PE_TILES, PACK):
+            make_rest(t)
 
         n_chunks = S // CHUNK
         out_rows = out_0.rearrange("(p t) j -> p t j", t=PACK)
         out_words = out_1[0].rearrange("p n t -> p (n t)").bitcast(I32)
         ow = sb("ow", [P, S], U32)
         osc = sb("osc", [P, S], U8)
-        zf = [sb("zf%d" % q, [P, PACK, CHUNK], F32) for q in range(n_chunks)]
-        zb = [sb("zb%d" % q, [P, CHUNK, PACK], BF16) for q in range(n_chunks)]
+        zb = {}
+        zf = {}
+        banks = {}
         zw = [sb("zw%d" % q, [P, CHUNK], U32) for q in range(n_chunks)]
         zs = [sb("zs%d" % q, [P, CHUNK], U8) for q in range(n_chunks)]
         of = [sb("of%d" % q, [P, PACK, CHUNK], F32) for q in range(n_chunks)]
         ob = [sb("ob%d" % q, [P, CHUNK, PACK], BF16) for q in range(n_chunks)]
 
-        def weave(engine_copy, dst, src):
-            engine_copy(dst[:].rearrange("p (c i) t -> p c t i", i=4), src[:].rearrange("p t (c i) -> p c t i", i=4))
+        def z_tile(q):
+            tag = "zb%d" % (q - 2) if q >= 2 else "turned%d_%d" % (PE_TILES - 1, q)
+            zf[q] = sb("zf%d" % q, [P, (PACK + 1) * CHUNK], F32, tag)
 
         def z_gather(q):
             cols = slice(q * CHUNK, (q + 1) * CHUNK)
             lcols = slice(q * CHUNK // LIST_ROWS, (q + 1) * CHUNK // LIST_ROWS)
+            if q not in zf:
+                z_tile(q)
             for t in range(PACK):
-                nc.vector.tensor_tensor(zf[q][:, t, :], eh[t][:].indirect(rt_l[:, lcols]), rest[t][:, cols], ADD)
-            weave(nc.scalar.copy if q < n_chunks - 1 else nc.vector.tensor_copy, zb[q], zf[q])
+                if t == PACK - 1 and q == n_chunks - 1:
+                    score(q - 1)
+                nc.vector.tensor_tensor(
+                    zf[q][:, t * CHUNK : (t + 1) * CHUNK], eh[t][:].indirect(rt_l[:, lcols]), rest[t][:, cols], SUB
+                )
+            if q == n_chunks - 2:
+                score(q - 1)
+                z_tile(q + 1)
+                zb[q] = zf[q + 1][:, (PACK - 1) * CHUNK :].bitcast(BF16)
+            else:
+                zb[q] = sb("zb%d" % q, [P, CHUNK * PACK], BF16)[:]
+            copy = nc.scalar.copy if q < n_chunks - 1 else nc.vector.tensor_copy
+            copy(
+                zb[q].rearrange("p (c i t) -> p c t i", i=4, t=PACK),
+                zf[q][:, : PACK * CHUNK].rearrange("p (t c i) -> p c t i", i=4, t=PACK),
+            )
 
         def score(q):
-            cols = slice(q * CHUNK, (q + 1) * CHUNK)
             nc.vector.quantize_mx(
-                out=zw[q][:].bitcast(FP8X4), scales=zs[q][:], in_=zb[q][:].rearrange("p j t -> p (j t)")
+                out=zw[q][:].bitcast(FP8X4), scales=zs[q][:], in_=zb[q]
             )
-            bank = psum.tile([P, PACK, CHUNK], F32, name="obank%d" % q, tag="bank%d" % q)
+            bank = psum.tile([P, PACK, CHUNK], F32, name="obank%d" % q, tag="bank%d" % (PACK + q))
             for t in range(PACK):
                 nc.tensor.matmul_mx(
                     out=bank[:, t, :],
@@ -198,9 +245,19 @@ def tile_picked_fdtd8_none_po_kernel(
                     start=True,
                     stop=True,
                 )
-            nc.scalar.activation(of[q][:], bank[:], COPY, scale=0.0625)
+            banks[q] = bank
+
+        def store_scores(q):
+            cols = slice(q * CHUNK, (q + 1) * CHUNK)
+            nc.scalar.activation(of[q][:], banks[q][:], COPY, scale=0.0625)
             nc.sync.dma_start(out_rows[:, :, cols], of[q][:])
-            weave(nc.scalar.copy if q < 1 else nc.vector.tensor_copy, ob[q], of[q])
+
+        def round_scores(q):
+            woven = banks[q][:].rearrange("p t j -> p j t")
+            if q == n_chunks - 1:
+                nc.vector.tensor_scalar(ob[q][:], woven, 0.0625, None, MULT)
+            else:
+                nc.scalar.activation(ob[q][:], woven, COPY, scale=0.0625)
 
         def hand_on(q):
             cols = slice(q * CHUNK, (q + 1) * CHUNK)
@@ -209,13 +266,22 @@ def tile_picked_fdtd8_none_po_kernel(
             )
             nc.sync.dma_start(out_words[:, cols], ow[:, cols].bitcast(I32))
 
-        for step in range(n_chunks + 2):
-            if step < n_chunks:
-                z_gather(step)
-            if 0 <= step - 1 < n_chunks:
-                score(step - 1)
-            if 0 <= step - 2 < n_chunks:
-                hand_on(step - 2)
+        z_gather(0)
+        z_gather(1)
+        score(0)
+        store_scores(0)
+        z_gather(2)
+        z_gather(3)
+        score(3)
+        round_scores(0)
+        store_scores(1)
+        round_scores(1)
+        round_scores(3)
+        store_scores(2)
+        round_scores(2)
+        store_scores(3)
+        for q in range(n_chunks):
+            hand_on(q)
         for q in range(QUADS):
             queue = nc.sync if q % 2 == 0 else nc.scalar
             queue.dma_start(out_2[0, 4 * q : 4 * q + 4, :].bitcast(I32), osc[32 * q : 32 * q + 4, :].bitcast(I32))

@@ -25,7 +25,7 @@ QUADS = 4
 LIST_ROWS = 16
 HALF = 256
 CHUNK = 128
-PE_TILES = 3
+PE_TILES = 2
 
 
 def tile_picked_fdtd8_none_po_kernel(
@@ -129,16 +129,12 @@ def tile_picked_fdtd8_none_po_kernel(
         two_w = gather_words("two_w", two_l)
         w2s_d = deal_bytes("w2s_d", w2s)
         c_ps = project(0, w2w_d, w2s_d, two_w, two_s)
-        cq = []
+        cwin = [sb("cwin%d" % t, [P, 2 * S], F32) for t in range(PACK)]
+        cq = [cwin[t][:, :S] for t in range(PACK)]
+        cn = [cwin[t][:, S:] for t in range(PACK)]
         for t in range(PACK):
-            w = sb("cq%d" % t, [P, S], F32)
-            nc.scalar.activation(w[:], c_ps[t][:], COPY, scale=gs_c[:, t : t + 1])
-            cq.append(w)
-        cn = []
-        for t in range(PE_TILES):
-            w = sb("cn%d" % t, [P, S], F32)
-            nc.scalar.activation(w[:], c_ps[t][:], COPY, scale=gs_n[:, t : t + 1])
-            cn.append(w)
+            nc.scalar.activation(cq[t], c_ps[t][:], COPY, scale=gs_c[:, t : t + 1])
+            nc.scalar.activation(cn[t], c_ps[t][:], COPY, scale=gs_n[:, t : t + 1])
         w1w_d = deal_fp4("w1w_d", w1w)
         offs_w = gather_words("offs_w", offs_l, "w2s")
         w1s_d = deal_bytes("w1s_d", w1s)
@@ -153,34 +149,33 @@ def tile_picked_fdtd8_none_po_kernel(
         rest = [sb("rest%d" % t, [P, S], F32) for t in range(PACK)]
 
         def make_own(t):
-            nc.vector.scalar_tensor_tensor(own[t][:], y_ps[t][:], gs_y[:, t : t + 1], cq[t][:], MULT, ADD)
+            nc.vector.scalar_tensor_tensor(own[t][:], y_ps[t][:], gs_y[:, t : t + 1], cq[t], MULT, ADD)
 
         def rest_by_transposes(t, h):
+            add_by_transposes("%d_%d" % (t, h), h, rest[t], cn[t], eh[t])
+
+        def add_by_transposes(name, h, dst, first, second):
             blocks = HALF // P
-            turned_ps = psum.tile([P, blocks, P], F32, name="turn%d_%d" % (t, h), tag="bank%d" % h)
+            turned_ps = psum.tile([P, blocks, P], F32, name="turn" + name, tag="bank%d" % h)
             for b in range(blocks):
                 cols = slice(h * HALF + b * P, h * HALF + (b + 1) * P)
-                nc.tensor.matmul(turned_ps[:, b, :], cn[t][:, cols], ident[:], is_transpose=True, start=True, stop=False)
-                nc.tensor.matmul(turned_ps[:, b, :], eh[t][:, cols], ident[:], is_transpose=True, start=False, stop=True)
-            turned = sb("turned%d_%d" % (t, h), [P, blocks, P], F32)
+                nc.tensor.matmul(turned_ps[:, b, :], first[:, cols], ident[:], is_transpose=True, start=True, stop=False)
+                nc.tensor.matmul(turned_ps[:, b, :], second[:, cols], ident[:], is_transpose=True, start=False, stop=True)
+            turned = sb("turned" + name, [P, blocks, P], F32)
             nc.scalar.copy(turned[:], turned_ps[:])
-            back_ps = psum.tile([P, blocks, P], F32, name="back%d_%d" % (t, h), tag="bank%d" % (2 + h))
+            back_ps = psum.tile([P, blocks, P], F32, name="back" + name, tag="bank%d" % (2 + h))
             for b in range(blocks):
                 nc.tensor.transpose(back_ps[:, b, :], turned[:, b, :], ident[:])
-            nc.scalar.copy(rest[t][:, h * HALF : (h + 1) * HALF], back_ps[:].rearrange("p b j -> p (b j)"))
+            nc.scalar.copy(dst[:, h * HALF : (h + 1) * HALF], back_ps[:].rearrange("p b j -> p (b j)"))
 
         def make_e(t):
-            for h in range(S // HALF):
-                cols = slice(h * HALF, (h + 1) * HALF)
-                lcols = slice(h * HALF // LIST_ROWS, (h + 1) * HALF // LIST_ROWS)
-                nc.vector.tensor_tensor(eh[t][:, cols], cq[t][:].indirect(lf_l[:, lcols]), own[t][:, cols], SUB)
-                if t < PE_TILES:
+            nc.vector.tensor_tensor(eh[t][:], cwin[t][:].indirect(lf_l[:]), own[t][:], SUB)
+            if t < PE_TILES:
+                for h in range(S // HALF):
                     rest_by_transposes(t, h)
 
         def make_rest(t):
-            for h in range(S // HALF):
-                cols = slice(h * HALF, (h + 1) * HALF)
-                nc.vector.scalar_tensor_tensor(rest[t][:, cols], cq[t][:, cols], 4.0, eh[t][:, cols], MULT, ADD)
+            nc.vector.tensor_tensor(rest[t][:], eh[t][:], cn[t], ADD)
 
         make_own(0)
         for t in range(PACK):
@@ -249,8 +244,11 @@ def tile_picked_fdtd8_none_po_kernel(
 
         def store_scores(q):
             cols = slice(q * CHUNK, (q + 1) * CHUNK)
-            nc.scalar.activation(of[q][:], banks[q][:], COPY, scale=0.0625)
-            nc.sync.dma_start(out_rows[:, :, cols], of[q][:])
+            pieces = 2 if q == n_chunks - 1 else 1
+            for i in range(pieces):
+                ts = slice(i * PACK // pieces, (i + 1) * PACK // pieces)
+                nc.scalar.activation(of[q][:, ts, :], banks[q][:, ts, :], COPY, scale=0.0625)
+                nc.sync.dma_start(out_rows[:, ts, cols], of[q][:, ts, :])
 
         def round_scores(q):
             woven = banks[q][:].rearrange("p t j -> p j t")

from contextlib import ExitStack

import concourse.mybir as mybir
from concourse.masks import make_identity

K, T, S, H, C = 512, 2048, 512, 512, 512
FLOPS = 2 * K * H * S * 2 + 2 * K * C * S

F32 = mybir.dt.float32
BF16 = mybir.dt.bfloat16
I32 = mybir.dt.int32
U32 = mybir.dt.uint32
U16 = mybir.dt.uint16
U8 = mybir.dt.uint8
FP8X4 = mybir.dt.float8_e4m3fn_x4
FP4X4 = mybir.dt.float4_e2m1fn_x4
MULT = mybir.AluOpType.mult
ADD = mybir.AluOpType.add
SUB = mybir.AluOpType.subtract
COPY = mybir.ActivationFunctionType.Copy

P = 128
PACK = 4
QUADS = 4
LIST_ROWS = 16
HALF = 256
CHUNK = 128
PE_TILES = 2


def tile_picked_fdtd8_none_po_kernel(
    tc, x_words, x_scales, w1_words, w1_scales, w2_words, w2_scales, gs, offs, two, lf, rt, cand, out_0, out_1, out_2
):
    nc = tc.nc
    with ExitStack() as ctx:
        keep = ctx.enter_context(tc.tile_pool(name="keep", bufs=1))
        psum = ctx.enter_context(tc.psum_pool(name="psum", bufs=1))

        def sb(name, shape, dtype, tag=None):
            return keep.tile(shape, dtype, name=name, tag=tag or name, align_bytes=64)

        def load_list(name, src):
            t = keep.tile([P, S // LIST_ROWS], U16, name=name)
            nc.sync.dma_start(t[:], src)
            return t

        def load_scales(name, src, width, zero_engine, queue):
            t = sb(name, [P, width], U8)
            share = width // len(zero_engine)
            for i, engine in enumerate(zero_engine):
                engine.memset(t[:, i * share : (i + 1) * share].bitcast(I32), 0)
            for q in range(QUADS):
                queue[q % len(queue)].dma_start(t[32 * q : 32 * q + 4, :].bitcast(I32), src[0, 4 * q : 4 * q + 4, :].bitcast(I32))
            return t

        def load_w_words(name, src, queue):
            t = sb(name, [P, 2 * H], U8)
            queue.dma_start(t[:].bitcast(I32), src[0].bitcast(I32))
            return t

        xs = load_scales("xs", x_scales, T, [nc.vector, nc.gpsimd], [nc.scalar, nc.sync])
        two_l = load_list("two_l", two)
        offs_l = load_list("offs_l", offs)
        w2w = load_w_words("w2w", w2_words, nc.scalar)
        xw = sb("xw", [P, T], U32)
        nc.sync.dma_start(xw[:].bitcast(I32), x_words[0].rearrange("p n t -> p (n t)").bitcast(I32))
        w2s = load_scales("w2s", w2_scales, H, [nc.vector], [nc.sync])
        w1w = load_w_words("w1w", w1_words, nc.sync)
        gs_t = sb("gs_t", [P, PACK], F32)
        nc.sync.dma_start(gs_t[:], gs.rearrange("(p t) o -> p (t o)", t=PACK))
        w1s = load_scales("w1s", w1_scales, H, [nc.vector], [nc.sync])
        cand_l = load_list("cand_l", cand)
        lf_l = load_list("lf_l", lf)
        rt_l = load_list("rt_l", rt)

        gs_c = sb("gs_c", [P, PACK], F32)
        gs_y = sb("gs_y", [P, PACK], F32)
        nc.scalar.mul(gs_c[:], gs_t[:], -0.25)
        gs_n = sb("gs_n", [P, PACK], F32)
        nc.scalar.mul(gs_y[:], gs_t[:], -0.5)
        nc.scalar.mul(gs_n[:], gs_t[:], -1.0)
        ident = sb("ident", [P, P], F32)
        make_identity(nc, ident[:])

        def gather_bytes(name, lst, tag=None):
            t = sb(name, [P, S], U8, tag)
            nc.vector.tensor_copy(t[:], xs[:].indirect(lst[:]))
            return t

        def gather_words(name, lst, tag=None):
            t = sb(name, [P, S], U32, tag)
            nc.vector.tensor_copy(t[:], xw[:].indirect(lst[:]))
            return t

        def deal_bytes(name, src):
            t = sb(name, [P, H], U8)
            nc.vector.tensor_copy(
                t[:].rearrange("p (t m) -> p t m", t=PACK), src[:].rearrange("p (m t) -> p t m", t=PACK)
            )
            return t

        def deal_fp4(name, src):
            t = sb(name, [P, 2 * H], U8)
            nc.vector.tensor_copy(
                t[:].bitcast(U16).rearrange("p (t m) -> p t m", t=PACK),
                src[:].bitcast(U16).rearrange("p (m t) -> p t m", t=PACK),
            )
            return t

        def project(tag0, w_words, w_scales, xg_words, xg_scales):
            banks = []
            for t in range(PACK):
                bank = psum.tile([P, S], F32, name="bank%d" % (tag0 + t), tag="bank%d" % (tag0 + t))
                nc.tensor.matmul_mx(
                    out=bank[:],
                    lhsT=w_words[:, 2 * P * t : 2 * P * (t + 1)].bitcast(FP4X4),
                    lhsT_scale=w_scales[:, P * t : P * (t + 1)],
                    rhs=xg_words[:].bitcast(FP8X4),
                    rhs_scale=xg_scales[:],
                    start=True,
                    stop=True,
                )
                banks.append(bank)
            return banks

        w2w_d = deal_fp4("w2w_d", w2w)
        two_s = gather_bytes("two_s", two_l)
        offs_s = gather_bytes("offs_s", offs_l)
        two_w = gather_words("two_w", two_l)
        w2s_d = deal_bytes("w2s_d", w2s)
        c_ps = project(0, w2w_d, w2s_d, two_w, two_s)
        cwin = [sb("cwin%d" % t, [P, 2 * S], F32) for t in range(PACK)]
        cq = [cwin[t][:, :S] for t in range(PACK)]
        cn = [cwin[t][:, S:] for t in range(PACK)]
        for t in range(PACK):
            nc.scalar.activation(cq[t], c_ps[t][:], COPY, scale=gs_c[:, t : t + 1])
            nc.scalar.activation(cn[t], c_ps[t][:], COPY, scale=gs_n[:, t : t + 1])
        w1w_d = deal_fp4("w1w_d", w1w)
        offs_w = gather_words("offs_w", offs_l, "w2s")
        w1s_d = deal_bytes("w1s_d", w1s)
        y_ps = project(PACK, w1w_d, w1s_d, offs_w, offs_s)
        cand_s = gather_bytes("cand_s", cand_l)
        cand_w_d = sb("cand_w_d", [P, C], U32)
        nc.vector.tensor_copy(cand_w_d[:].rearrange("p (t m) -> p m t", t=PACK), xw[:].indirect(cand_l[:]))
        cand_s_d = deal_bytes("cand_s_d", cand_s)

        own = [sb("own%d" % t, [P, S], F32) for t in range(PACK)]
        eh = [sb("eh%d" % t, [P, S], F32) for t in range(PACK)]
        rest = [sb("rest%d" % t, [P, S], F32) for t in range(PACK)]

        def make_own(t):
            nc.vector.scalar_tensor_tensor(own[t][:], y_ps[t][:], gs_y[:, t : t + 1], cq[t], MULT, ADD)

        def rest_by_transposes(t, h):
            add_by_transposes("%d_%d" % (t, h), h, rest[t], cn[t], eh[t])

        def add_by_transposes(name, h, dst, first, second):
            blocks = HALF // P
            turned_ps = psum.tile([P, blocks, P], F32, name="turn" + name, tag="bank%d" % h)
            for b in range(blocks):
                cols = slice(h * HALF + b * P, h * HALF + (b + 1) * P)
                nc.tensor.matmul(turned_ps[:, b, :], first[:, cols], ident[:], is_transpose=True, start=True, stop=False)
                nc.tensor.matmul(turned_ps[:, b, :], second[:, cols], ident[:], is_transpose=True, start=False, stop=True)
            turned = sb("turned" + name, [P, blocks, P], F32)
            nc.scalar.copy(turned[:], turned_ps[:])
            back_ps = psum.tile([P, blocks, P], F32, name="back" + name, tag="bank%d" % (2 + h))
            for b in range(blocks):
                nc.tensor.transpose(back_ps[:, b, :], turned[:, b, :], ident[:])
            nc.scalar.copy(dst[:, h * HALF : (h + 1) * HALF], back_ps[:].rearrange("p b j -> p (b j)"))

        def make_e(t):
            nc.vector.tensor_tensor(eh[t][:], cwin[t][:].indirect(lf_l[:]), own[t][:], SUB)
            if t < PE_TILES:
                for h in range(S // HALF):
                    rest_by_transposes(t, h)

        def make_rest(t):
            nc.vector.tensor_tensor(rest[t][:], eh[t][:], cn[t], ADD)

        make_own(0)
        for t in range(PACK):
            if t + 1 < PACK:
                make_own(t + 1)
            make_e(t)
        for t in range(PE_TILES, PACK):
            make_rest(t)

        n_chunks = S // CHUNK
        out_rows = out_0.rearrange("(p t) j -> p t j", t=PACK)
        out_words = out_1[0].rearrange("p n t -> p (n t)").bitcast(I32)
        ow = sb("ow", [P, S], U32)
        osc = sb("osc", [P, S], U8)
        zb = {}
        zf = {}
        banks = {}
        zw = [sb("zw%d" % q, [P, CHUNK], U32) for q in range(n_chunks)]
        zs = [sb("zs%d" % q, [P, CHUNK], U8) for q in range(n_chunks)]
        of = [sb("of%d" % q, [P, PACK, CHUNK], F32) for q in range(n_chunks)]
        ob = [sb("ob%d" % q, [P, CHUNK, PACK], BF16) for q in range(n_chunks)]

        def z_tile(q):
            tag = "zb%d" % (q - 2) if q >= 2 else "turned%d_%d" % (PE_TILES - 1, q)
            zf[q] = sb("zf%d" % q, [P, (PACK + 1) * CHUNK], F32, tag)

        def z_gather(q):
            cols = slice(q * CHUNK, (q + 1) * CHUNK)
            lcols = slice(q * CHUNK // LIST_ROWS, (q + 1) * CHUNK // LIST_ROWS)
            if q not in zf:
                z_tile(q)
            for t in range(PACK):
                if t == PACK - 1 and q == n_chunks - 1:
                    score(q - 1)
                nc.vector.tensor_tensor(
                    zf[q][:, t * CHUNK : (t + 1) * CHUNK], eh[t][:].indirect(rt_l[:, lcols]), rest[t][:, cols], SUB
                )
            if q == n_chunks - 2:
                score(q - 1)
                z_tile(q + 1)
                zb[q] = zf[q + 1][:, (PACK - 1) * CHUNK :].bitcast(BF16)
            else:
                zb[q] = sb("zb%d" % q, [P, CHUNK * PACK], BF16)[:]
            copy = nc.scalar.copy if q < n_chunks - 1 else nc.vector.tensor_copy
            copy(
                zb[q].rearrange("p (c i t) -> p c t i", i=4, t=PACK),
                zf[q][:, : PACK * CHUNK].rearrange("p (t c i) -> p c t i", i=4, t=PACK),
            )

        def score(q):
            nc.vector.quantize_mx(
                out=zw[q][:].bitcast(FP8X4), scales=zs[q][:], in_=zb[q]
            )
            bank = psum.tile([P, PACK, CHUNK], F32, name="obank%d" % q, tag="bank%d" % (PACK + q))
            for t in range(PACK):
                nc.tensor.matmul_mx(
                    out=bank[:, t, :],
                    lhsT=cand_w_d[:, P * t : P * (t + 1)].bitcast(FP8X4),
                    lhsT_scale=cand_s_d[:, P * t : P * (t + 1)],
                    rhs=zw[q][:].bitcast(FP8X4),
                    rhs_scale=zs[q][:],
                    start=True,
                    stop=True,
                )
            banks[q] = bank

        def store_scores(q):
            cols = slice(q * CHUNK, (q + 1) * CHUNK)
            pieces = 2 if q == n_chunks - 1 else 1
            for i in range(pieces):
                ts = slice(i * PACK // pieces, (i + 1) * PACK // pieces)
                nc.scalar.activation(of[q][:, ts, :], banks[q][:, ts, :], COPY, scale=0.0625)
                nc.sync.dma_start(out_rows[:, ts, cols], of[q][:, ts, :])

        def round_scores(q):
            woven = banks[q][:].rearrange("p t j -> p j t")
            if q == n_chunks - 1:
                nc.vector.tensor_scalar(ob[q][:], woven, 0.0625, None, MULT)
            else:
                nc.scalar.activation(ob[q][:], woven, COPY, scale=0.0625)

        def hand_on(q):
            cols = slice(q * CHUNK, (q + 1) * CHUNK)
            nc.vector.quantize_mx(
                out=ow[:, cols].bitcast(FP8X4), scales=osc[:, cols], in_=ob[q][:].rearrange("p j t -> p (j t)")
            )
            nc.sync.dma_start(out_words[:, cols], ow[:, cols].bitcast(I32))

        z_gather(0)
        z_gather(1)
        score(0)
        store_scores(0)
        z_gather(2)
        z_gather(3)
        score(3)
        round_scores(0)
        store_scores(1)
        round_scores(1)
        round_scores(3)
        store_scores(2)
        round_scores(2)
        store_scores(3)
        for q in range(n_chunks):
            hand_on(q)
        for q in range(QUADS):
            queue = nc.sync if q % 2 == 0 else nc.scalar
            queue.dma_start(out_2[0, 4 * q : 4 * q + 4, :].bitcast(I32), osc[32 * q : 32 * q + 4, :].bitcast(I32))
